import numpy as np
import ml_dtypes


def mxq(x, axis, fmt="e4m3"):
    dtype, down = {"e4m3": (ml_dtypes.float8_e4m3fn, 7), "e5m2": (ml_dtypes.float8_e5m2, 14)}[fmt]
    v = np.moveaxis(np.asarray(x, np.float32).astype(ml_dtypes.bfloat16).astype(np.float64), axis, -1)
    blocks = v.reshape(v.shape[:-1] + (-1, 32))
    amax = np.abs(blocks).max(-1, keepdims=True)
    byte = np.maximum(np.where(amax > 0, np.frexp(amax)[1] - 1 + 127, 0) - down, 1)
    scale = np.exp2(byte - 127.0)
    codes = (blocks / scale).astype(np.float32).astype(dtype).astype(np.float64)
    return np.moveaxis((codes * scale).reshape(v.shape), -1, axis)


WIDE = False


def mx_kscale(k):
    if not WIDE:
        return np.ones(k)
    levels = np.array([10, -10, 5, -5, 0])
    if k % 512:
        return np.exp2(np.random.permutation(np.resize(levels, k // 32))).repeat(32)
    a = np.empty((k // 512, 16))
    for p in range(k // 512):
        a[p, :8] = np.random.permutation(np.resize(levels, 8))
        for g in range(8):
            far = levels[np.abs(levels - a[p, g]) >= 10]
            a[p, g + 8] = far[np.random.randint(len(far))]
    return np.exp2(a.ravel()).repeat(32)


def f64(x):
    return np.asarray(x).astype(np.float64)


def striped(idx):
    return np.tile(idx.reshape(-1, 16).T, (8, 1)).astype(np.uint16)


def unstriped(offs):
    return offs[:16].T.reshape(-1).astype(np.int64)


def pack_weight(w):
    k, n = w.shape
    w = f64(np.asarray(w, np.float32).astype(ml_dtypes.bfloat16)).reshape(k // 32, 32, n)
    amax = np.abs(w).max(1)
    byte = np.clip(np.where(amax > 0, np.frexp(amax)[1] - 1 + 127 - 7, 1), 1, 254)
    scaled = (w * np.exp2(127.0 - byte)[:, None, :]).reshape(k, n).astype(np.float32)
    words = np.ascontiguousarray(scaled.reshape(k // 512, 128, 4, n).transpose(0, 1, 3, 2)).astype(ml_dtypes.float8_e4m3fn).view(np.uint8)
    return words, np.ascontiguousarray(byte.astype(np.uint8).reshape(k // 512, 16, n))


def unpack_weight(words, scales):
    g, p, n, _ = words.shape
    vals = np.ascontiguousarray(words).view(ml_dtypes.float8_e4m3fn).astype(np.float64) * np.repeat(np.exp2(scales.astype(np.float64) - 127.0), 8, axis=1)[..., None]
    return vals.transpose(0, 1, 3, 2).reshape(g * 512, n)


K, T, S, N, W, G = 512, 2048, 512, 128, 1024, 2048
P = 2 ** 7


def setup_inputs():
    n = np.random.standard_normal
    s = mx_kscale(K)[:, None]
    packed_xT = pack_weight(n((K, T)) * s)
    packed_eT = pack_weight(n((K, W)) * s)
    packed_dT = pack_weight(n((K, G)) * s)
    return {
        "x_words": packed_xT[0],
        "x_scales": packed_xT[1],
        "e_words": packed_eT[0],
        "e_scales": packed_eT[1],
        "d_words": packed_dT[0],
        "d_scales": packed_dT[1],
        "att0": (np.tile(n(T) * 0.7, (P, 1))).astype(np.float32),
        "att1": (np.tile(n(T) * 0.7, (P, 1))).astype(np.float32),
        "att2": (np.tile(n(T) * 0.7, (P, 1))).astype(np.float32),
        "w1": (n((K, N)) / np.sqrt(K) / s).astype(np.float32),
        "w2": (n((K, N)) / np.sqrt(K) / s).astype(np.float32),
        "w3": (n((K, N)) / np.sqrt(K) / s).astype(np.float32),
        "offs": striped(np.random.permutation(T)[:S]),
        "shop": striped(np.random.permutation(W)[:S]),
        "brand": striped(np.random.permutation(G)[:S]),
    }


def reference(x_words, x_scales, e_words, e_scales, d_words, d_scales, att0, att1, att2, w1, w2, w3, offs, shop, brand):
    xq = unpack_weight(x_words, x_scales)[:, unstriped(offs)]
    y0 = mxq(f64(w1), 0, "e4m3").T @ xq
    a0 = np.exp(f64(att0)[:1][:, unstriped(offs)])
    e_shop = unpack_weight(e_words, e_scales)[:, unstriped(shop)]
    y1 = mxq(f64(w2), 0, "e4m3").T @ e_shop
    a1 = np.exp(f64(att1)[:1][:, unstriped(offs)])
    d_brand = unpack_weight(d_words, d_scales)[:, unstriped(brand)]
    y2 = mxq(f64(w3), 0, "e4m3").T @ d_brand
    a2 = np.exp(f64(att2)[:1][:, unstriped(offs)])
    num = y0 * a0 + y1 * a1 + y2 * a2
    den = a0 + a1 + a2
    return np.tanh(num / den)

from contextlib import ExitStack

import concourse.mybir as mybir

F32 = mybir.dt.float32
BF16 = mybir.dt.bfloat16
I32 = mybir.dt.int32
U32 = mybir.dt.uint32
U16 = mybir.dt.uint16
U8 = mybir.dt.uint8
FP8X4 = mybir.dt.float8_e4m3fn_x4
ACT = mybir.ActivationFunctionType
ALU = mybir.AluOpType

P = 128
PACK = 4
K = 512
S = 512
N = 128
BLOCKS = S // P
LIST_COLS = P // 16
ATT_ROW0 = 12
ATT_STEP = 4

FLOPS = 3 * 2 * K * N * S
BYTES = K * (2048 + 1024 + 2048) + 16 * (2048 + 1024 + 2048) + 3 * 2048 * 4 + 3 * K * N * 4 + 3 * P * 32 * 2 + N * S * 4


def tile_picked_yeges_tanh_p_kernel(
    tc, x_words, x_scales, e_words, e_scales, d_words, d_scales, att0, att1, att2, w1, w2, w3, offs, shop, brand, out
):
    nc = tc.nc
    with ExitStack() as ctx:
        keep = ctx.enter_context(tc.tile_pool(name="keep", bufs=1))
        psum = ctx.enter_context(tc.psum_pool(name="psum", bufs=1))

        lists, word_win, scale_win, w_raw = {}, {}, {}, {}
        att_win = keep.tile([P, att0.shape[1]], F32, name="att_win")

        def load_list(name, src):
            lists[name] = keep.tile([P, S // 16], U16, name=name + "_list")
            nc.sync.dma_start(lists[name][:], src)

        def load_words(name, src, tag):
            word_win[name] = keep.tile([P, src.shape[2]], I32, name=name + "_word_win", tag=tag)
            nc.sync.dma_start(word_win[name][:], src[0].rearrange("p n t -> p (n t)").bitcast(I32))

        def scale_words(name, src, tag):
            scale_win[name] = keep.tile([P, src.shape[2]], U8, name=name + "_scale_win", tag=tag)
            return scale_win[name][:].bitcast(I32), src[0].bitcast(I32)

        def load_scale_rows(tile_words, rows, row0, q):
            nc.sync.dma_start(tile_words[32 * q + row0 : 32 * q + row0 + 4, :], rows[4 * q : 4 * q + 4, :])

        def load_weight(name, src, tag):
            w_raw[name] = keep.tile([P, PACK, N], F32, name=name + "_w_raw", tag=tag)
            nc.sync.dma_start(w_raw[name][:], src.rearrange("(p t) m -> p t m", t=PACK))

        e_tile, e_rows = scale_words("e", e_scales, "e_scales_then_d_words")
        x_tile, x_rows = scale_words("x", x_scales, "x_scales")
        zeros = keep.tile([P, P], F32, name="zeros", tag="zeros_then_x_words_then_rden")
        ident = keep.tile([P, P], F32, name="ident")

        half = att0.shape[1] // 2
        nc.gpsimd.memset(e_tile, 0)
        nc.gpsimd.memset(att_win[:, :half], 0.0)
        nc.vector.memset(att_win[:, half:], 0.0)
        nc.gpsimd.memset(zeros[:], 0.0)
        nc.gpsimd.affine_select(
            out=ident[:], in_=zeros[:], pattern=[[-1, P]], compare_op=ALU.not_equal, fill=1.0, base=0, channel_multiplier=1
        )
        nc.gpsimd.memset(x_tile, 0)

        load_list("e", shop)
        load_list("x", offs)
        load_list("d", brand)
        load_words("e", e_words, "e_words_then_w3")
        for q in range(4):
            load_scale_rows(e_tile, e_rows, 0, q)
        load_weight("e", w2, "w2_then_d_scales")
        load_weight("x", w1, "w1")
        for i, att in enumerate((att0, att1, att2)):
            row = ATT_ROW0 + ATT_STEP * i
            nc.sync.dma_start(att_win[row : row + 1, :], att[0:1, :])
        load_words("x", x_words, "zeros_then_x_words_then_rden")
        for q in range(4):
            load_scale_rows(x_tile, x_rows, 4, q)

        att_exp = keep.tile([P, S], F32, name="att_exp")
        nc.scalar.activation(out=att_exp[:], in_=att_win[:].indirect(lists["x"][:]), func=ACT.Exp)
        att_t = psum.tile([P, BLOCKS, P], F32, name="att_t", tag="bank_a")
        for b in range(BLOCKS):
            nc.tensor.transpose(att_t[:, b, :], att_exp[:, b * P : (b + 1) * P], ident[:])
        a_cols = att_t[:, :, ATT_ROW0 : ATT_ROW0 + 3 * ATT_STEP : ATT_STEP]
        den = keep.tile([P, BLOCKS], F32, name="den")
        a_t = keep.tile([P, BLOCKS, 3], F32, name="a_t")
        for b in range(BLOCKS):
            nc.scalar.activation(out=a_t[:, b, :], in_=a_cols[:, b, :], func=ACT.Copy, accum_out=den[:, b : b + 1])
        alpha = keep.tile([P, BLOCKS, 3], F32, name="alpha")

        codes, code_scales, w_codes, w_scales, scaled = {}, {}, {}, {}, {}

        def quantize_weight(name):
            grouped = keep.tile([P, N, PACK], BF16, name=name + "_w_grouped", tag=name + "_w_grouped", align_bytes=64)
            nc.scalar.activation(out=grouped[:], in_=w_raw[name][:].rearrange("p t m -> p m t"), func=ACT.Copy)
            w_codes[name] = keep.tile([P, N], U32, name=name + "_w_codes", align_bytes=64)
            w_scales[name] = keep.tile([P, N], U8, name=name + "_w_scales", align_bytes=64)
            nc.vector.quantize_mx(
                out=w_codes[name][:].bitcast(FP8X4),
                scales=w_scales[name][:],
                in_=grouped[:].rearrange("p m t -> p (m t)"),
            )

        def gather_scales(name, b0, b1, tag):
            picked = keep.tile([P, (b1 - b0) * P], U8, name="%s_code_scales_%d" % (name, b0), tag=tag, align_bytes=64)
            nc.vector.tensor_copy(
                picked[:], scale_win[name][:].indirect(lists[name][:, b0 * LIST_COLS : b1 * LIST_COLS])
            )
            for b in range(b0, b1):
                code_scales[name, b] = picked[:, (b - b0) * P : (b - b0 + 1) * P]

        def gather_words(name, b0, b1, tag):
            picked = keep.tile([P, (b1 - b0) * P], U32, name="%s_codes_%d" % (name, b0), tag=tag, align_bytes=64)
            nc.vector.tensor_copy(
                picked[:], word_win[name][:].bitcast(U32).indirect(lists[name][:, b0 * LIST_COLS : b1 * LIST_COLS])
            )
            for b in range(b0, b1):
                codes[name, b] = picked[:, (b - b0) * P : (b - b0 + 1) * P]

        def project(name, row0, acc, b0, b1):
            for b in range(b0, b1):
                nc.tensor.matmul_mx(
                    out=acc[:, b - b0, :],
                    lhsT=codes[name, b].bitcast(FP8X4),
                    lhsT_scale=code_scales[name, b][row0:P, :],
                    rhs=w_codes[name][:].bitcast(FP8X4),
                    rhs_scale=w_scales[name][:],
                    start=True,
                    stop=True,
                )

        def weigh(name, col, acc, b, on_vector):
            scaled[name, b] = keep.tile([P, N], F32, name="%s_scaled_%d" % (name, b))
            if on_vector:
                nc.vector.tensor_scalar_mul(scaled[name, b][:], acc, alpha[:, b, col : col + 1])
            else:
                nc.scalar.activation(out=scaled[name, b][:], in_=acc, func=ACT.Copy, scale=alpha[:, b, col : col + 1])

        def add_turned(total, name, b, first, last):
            nc.tensor.matmul(total, scaled[name, b][:], ident[:], start=first, stop=last, is_transpose=True)

        gather_words("e", 0, BLOCKS, "e_codes")
        load_weight("d", w3, "e_words_then_w3")
        gather_scales("e", 0, BLOCKS, "e_code_scales")
        load_words("d", d_words, "e_scales_then_d_words")
        quantize_weight("e")
        d_tile, d_rows = scale_words("d", d_scales, "w2_then_d_scales")
        nc.gpsimd.memset(d_tile, 0)
        for q in range(4):
            load_scale_rows(d_tile, d_rows, 8, q)
        quantize_weight("x")
        acc_e = psum.tile([P, BLOCKS, N], F32, name="acc_e")
        project("e", 0, acc_e, 0, BLOCKS)
        gather_words("x", 0, BLOCKS, "x_codes")
        rden = keep.tile([P, BLOCKS], F32, name="rden", tag="zeros_then_x_words_then_rden")
        nc.vector.reciprocal(rden[:], den[:])
        gather_scales("x", 0, BLOCKS, "x_code_scales")
        quantize_weight("d")
        for b in range(BLOCKS):
            nc.scalar.activation(out=alpha[:, b, :], in_=a_t[:, b, :], func=ACT.Copy, scale=rden[:, b : b + 1])
        totals = [psum.tile([P, P], F32, name="total_%d" % b) for b in range(BLOCKS)]
        for b in range(BLOCKS):
            weigh("e", 1, acc_e[:, b, :], b, False)
            add_turned(totals[b][:], "e", b, True, False)
        acc_x = psum.tile([P, BLOCKS, N], F32, name="acc_x")
        project("x", 4, acc_x, 0, BLOCKS)
        for b in range(BLOCKS):
            weigh("x", 0, acc_x[:, b, :], b, False)
            add_turned(totals[b][:], "x", b, False, False)
        gather_words("d", 0, BLOCKS, "d_codes")

        for b0, on_vector, queue in ((0, False, nc.sync), (2, True, nc.scalar)):
            gather_scales("d", b0, b0 + 2, "d_code_scales_%d" % b0)
            acc_d = psum.tile([P, 2, N], F32, name="acc_d_%d" % b0, tag="bank_a" if b0 == 0 else "acc_d_hi")
            project("d", 8, acc_d, b0, b0 + 2)
            result = keep.tile([P, 2 * P], F32, name="result_%d" % b0)
            for b in (b0, b0 + 1):
                weigh("d", 2, acc_d[:, b - b0, :], b, on_vector)
                add_turned(totals[b][:], "d", b, False, True)
            for b in (b0, b0 + 1):
                nc.scalar.activation(out=result[:, (b - b0) * P : (b - b0 + 1) * P], in_=totals[b][:], func=ACT.Tanh)
            queue.dma_start(out[:, b0 * P : (b0 + 2) * P], result[:])
